import numpy as np, ml_dtypes
CORES = [17,57,65,89,97,121]
N = 6
GR, GC = 2, 3
L, KA, KB, F = 12, 4, 6, 64
def setup_inputs(rng):
    return {"a": rng.standard_normal((N, 128, KA * 128), dtype=np.float32).astype(ml_dtypes.bfloat16), "b": rng.standard_normal((N, 128, KB * F), dtype=np.float32).astype(ml_dtypes.bfloat16)}
def setup_inputs_big(rng):
    d = setup_inputs(rng)
    for k in ("a", "b"): d[k] = (d[k].astype(np.float32) * 1024.0).astype(d[k].dtype)
    return d
def setup_inputs_small(rng):
    d = setup_inputs(rng)
    for k in ("a", "b"): d[k] = (d[k].astype(np.float32) * (1 / 1024.0)).astype(d[k].dtype)
    return d
def setup_inputs_apart(rng):
    d = setup_inputs(rng)
    f = (10.0 ** rng.permutation(np.linspace(-1.5, 1.5, N))).astype(np.float32).reshape(N, 1, 1)
    for k in ("a", "b"): d[k] = (d[k].astype(np.float32) * f).astype(d[k].dtype)
    return d
def reference(a, b):
    A, B = a.astype(np.float64), b.astype(np.float64)
    y = np.zeros((N, 128, F))
    for i in range(GR):
        for j in range(GC):
            for k in range(L):
                At = A[i * GC + k // KA][:, 128 * (k % KA):128 * (k % KA) + 128]
                Bt = B[(k // KB) * GC + j][:, F * (k % KB):F * (k % KB) + F]
                y[i * GC + j] += At.T @ Bt
    return {"y": y.astype(ml_dtypes.bfloat16 if a.dtype != np.float64 else np.float64)}

@@ -1,0 +1,141 @@
+from concourse.bass import DstId, RemoteDMATransfer
+
+GR, GC = 2, 3
+L, KA, KB, F = 12, 4, 6, 64
+P = 128
+AW, BW = KA * P, KB * F
+
+NE_ON = 8
+NE_OFF = 8
+
+SCRATCH = {
+    "a_d": ("dram", [P, AW], "bfloat16"),
+    "b_d": ("dram", [P, BW], "bfloat16"),
+    "A_all": ("sbuf", [P, L * P], "bfloat16"),
+    "B_all": ("sbuf", [P, L * F], "bfloat16"),
+    "acc": ("psum", [P, F], "float32"),
+    "y_s": ("sbuf", [P, F], "bfloat16"),
+}
+SEMAPHORES = ["la", "lb", "las", "lbs", "rx", "ra0", "ra1", "ra2", "rb", "sent", "mm", "cp", "st"]
+
+
+def _engines(mask, n, skip=0):
+    bits = [e for e in range(mask.bit_length()) if (mask >> e) & 1]
+    bits = bits[len(bits) - skip - n:len(bits) - skip]
+    return sum(1 << e for e in bits)
+
+
+def _flows(cores, topo):
+    everyone = range(topo.CHIPS * topo.CORES_PER_CHIP)
+    flows = []
+    for s, src in enumerate(cores):
+        i, j = divmod(s, GC)
+        wanted = [("a", i * GC + jj, min(j, jj) == 0) for jj in range(GC) if jj != j]
+        wanted.append(("b", (1 - i) * GC + j, j == GC - 1))
+        taken = []
+        for kind, d, other_die in wanted:
+            dst = cores[d]
+            if topo.may_write(src, dst):
+                flows.append((kind, s, d, None))
+                continue
+            able = [h for h in everyone
+                    if topo.chip(h) == topo.chip(src) and h not in cores and h not in taken
+                    and topo.may_write(h, dst)]
+            liked = [h for h in able if (topo.die(h) != topo.die(src)) == other_die]
+            relay = (liked or able)[0]
+            taken.append(relay)
+            flows.append((kind, s, d, relay))
+    return flows
+
+
+def _landing(T, kind, s):
+    i, j = divmod(s, GC)
+    if kind == "a":
+        return T.A_all[:, AW * j:AW * (j + 1)], T.sem["ra%d" % j]
+    return T.B_all[:, BW * i:BW * (i + 1)], T.sem.rb
+
+
+def rank_program(g, core, T, topo):
+    cores = list(T.cores)
+    flows = _flows(cores, topo)
+    sem = T.sem
+    rank = T.rank_of(core)
+
+    if rank is None:
+        for kind, s, d, relay in flows:
+            if relay != core:
+                continue
+            dst = cores[d]
+            out, arrived = _landing(T, kind, s)
+            rid, pid, _ = topo.addr(dst)
+            g.wait_ge(sem.rx, NE_ON)
+            g.remote_dma(out_ap=out, in_ap=(T.a_d if kind == "a" else T.b_d)[:, :], remote_sem=arrived,
+                         local_sem=sem.sent, pid=pid, routing_id=rid,
+                         dma_engine_mask=_engines(topo.mask(core, dst), NE_OFF))
+            g.wait_ge(sem.sent, NE_OFF)
+        return
+
+    i, j = divmod(rank, GC)
+    mine = [f for f in flows if f[1] == rank]
+
+    g.sync.dma_start(T.a_d[:, :], T.a[:, :]).then_inc(sem.la, 16)
+    g.scalar.dma_start(T.b_d[:, :], T.b[:, :]).then_inc(sem.lb, 16)
+    g.sync.dma_start(T.A_all[:, AW * j:AW * (j + 1)], T.a[:, :]).then_inc(sem.las, 16)
+    g.scalar.dma_start(T.B_all[:, BW * i:BW * (i + 1)], T.b[:, :]).then_inc(sem.lbs, 16)
+
+    sent = 0
+    g.wait_ge(sem.la, 16)
+    hand = []
+    for n, (kind, s, d, relay) in enumerate([f for f in mine if f[0] == "a" and f[3] is not None]):
+        rid, pid, _ = topo.addr(relay)
+        hand.append(RemoteDMATransfer(dst_ids=[DstId(rid=rid, pnc=pid)],
+                                      dma_engine_mask=_engines(topo.mask(core, relay), NE_ON, skip=n * NE_ON),
+                                      remote_sem=sem.rx, src=T.a_d[:, :], dst=T.a_d[:, :]))
+        sent += NE_ON
+    g.remote_dma_fused(hand, local_sem=sem.sent)
+    g.wait_ge(sem.lb, 16)
+    for kind, s, d, relay in [f for f in mine if f[0] == "b"]:
+        rid, pid, _ = topo.addr(relay)
+        g.remote_dma(out_ap=T.b_d[:, :], in_ap=T.b_d[:, :], remote_sem=sem.rx, local_sem=sem.sent, pid=pid,
+                     routing_id=rid, dma_engine_mask=_engines(topo.mask(core, relay), NE_ON))
+        sent += NE_ON
+    for kind, s, d, relay in [f for f in mine if f[3] is None]:
+        dst = cores[d]
+        out, arrived = _landing(T, kind, s)
+        rid, pid, _ = topo.addr(dst)
+        g.remote_dma(out_ap=out, in_ap=T.a_d[:, :], remote_sem=arrived, local_sem=sem.sent, pid=pid,
+                     routing_id=rid, dma_engine_mask=_engines(topo.mask(core, dst), NE_OFF))
+        sent += NE_OFF
+
+    how = {}
+    for kind, s, d, relay in flows:
+        if d == rank:
+            how[(kind, s)] = relay
+    need = {}
+    for k in range(L):
+        sa, sb = i * GC + k // KA, (k // KB) * GC + j
+        stage_a = 0 if sa == rank else (1 if how[("a", sa)] is None else 2)
+        stage_b = 0 if sb == rank else 3
+        need[k] = (max(stage_a, stage_b), k, sa, sb)
+    order = sorted(range(L), key=lambda k: need[k][:2])
+    waited = []
+    for n, k in enumerate(order):
+        _, _, sa, sb = need[k]
+        for kind, s in (("a", sa), ("b", sb)):
+            if (kind, s) in waited:
+                continue
+            waited.append((kind, s))
+            if s == rank:
+                g.tensor.wait_ge(sem.las if kind == "a" else sem.lbs, 16)
+            else:
+                g.tensor.wait_ge(_landing(T, kind, s)[1], NE_OFF)
+        mm = g.tensor.matmul(T.acc[:, :], T.A_all[:, P * k:P * (k + 1)], T.B_all[:, F * k:F * (k + 1)],
+                             n == 0, n == L - 1)
+    mm.then_inc(sem.mm, 1)
+
+    g.vector.wait_ge(sem.mm, 1)
+    g.vector.tensor_copy(T.y_s[:, :], T.acc[:, :]).then_inc(sem.cp, 1)
+    g.sync.wait_ge(sem.cp, 1)
+    g.sync.dma_start(T.y[:, :], T.y_s[:, :]).then_inc(sem.st, 16)
+    g.sync.wait_ge(sem.st, 16)
+    g.wait_ge(sem.sent, sent)

@@ -4,25 +4,29 @@ GR, GC = 2, 3
 L, KA, KB, F = 12, 4, 6, 64
 P = 128
 AW, BW = KA * P, KB * F
+HEAD = 64
+CUT = {"a": (0, HEAD, AW), "b": (0, HEAD, BW)}
 
-NE_ON = 8
+NE_IN = (4, 8)
 NE_OFF = 8
 
 SCRATCH = {
-    "a_d": ("dram", [P, AW], "bfloat16"),
-    "b_d": ("dram", [P, BW], "bfloat16"),
+    "a0_d": ("dram", [P, HEAD], "bfloat16"),
+    "a1_d": ("dram", [P, AW - HEAD], "bfloat16"),
+    "b0_d": ("dram", [P, HEAD], "bfloat16"),
+    "b1_d": ("dram", [P, BW - HEAD], "bfloat16"),
     "A_all": ("sbuf", [P, L * P], "bfloat16"),
     "B_all": ("sbuf", [P, L * F], "bfloat16"),
     "acc": ("psum", [P, F], "float32"),
     "y_s": ("sbuf", [P, F], "bfloat16"),
 }
-SEMAPHORES = ["la", "lb", "las", "lbs", "rx", "ra0", "ra1", "ra2", "rb", "sent", "mm", "cp", "st"]
+SEMAPHORES = ["la0", "la1", "lb0", "lb1", "las", "lbs", "rx0", "rx1",
+              "ra0h", "ra1h", "ra2h", "ra0", "ra1", "ra2", "rbh", "rb", "sent", "mm", "cp", "st"]
 
 
-def _engines(mask, n, skip=0):
-    bits = [e for e in range(mask.bit_length()) if (mask >> e) & 1]
-    bits = bits[len(bits) - skip - n:len(bits) - skip]
-    return sum(1 << e for e in bits)
+def _pick(mask, n, used=0):
+    bits = [e for e in range(mask.bit_length()) if (mask >> e) & 1 and not (used >> e) & 1]
+    return sum(1 << e for e in bits[len(bits) - n:])
 
 
 def _flows(cores, topo):
@@ -38,9 +42,14 @@ def _flows(cores, topo):
             if topo.may_write(src, dst):
                 flows.append((kind, s, d, None))
                 continue
-            able = [h for h in everyone
-                    if topo.chip(h) == topo.chip(src) and h not in cores and h not in taken
-                    and topo.may_write(h, dst)]
+            if kind == "b" and 0 < j < GC - 1:
+                able = [h for h in everyone
+                        if topo.mates(topo.chip(h), topo.chip(dst)) and h not in cores
+                        and topo.may_write(src, h) and topo.may_write(h, dst)]
+            else:
+                able = [h for h in everyone
+                        if topo.chip(h) == topo.chip(src) and h not in cores and h not in taken
+                        and topo.may_write(h, dst)]
             liked = [h for h in able if (topo.die(h) != topo.die(src)) == other_die]
             relay = (liked or able)[0]
             taken.append(relay)
@@ -48,11 +57,13 @@ def _flows(cores, topo):
     return flows
 
 
-def _landing(T, kind, s):
+def _landing(T, kind, s, piece):
     i, j = divmod(s, GC)
+    lo, hi = (CUT[kind][0], CUT[kind][2]) if piece is None else (CUT[kind][piece], CUT[kind][piece + 1])
+    tail = "h" if piece == 0 else ""
     if kind == "a":
-        return T.A_all[:, AW * j:AW * (j + 1)], T.sem["ra%d" % j]
-    return T.B_all[:, BW * i:BW * (i + 1)], T.sem.rb
+        return T.A_all[:, AW * j + lo:AW * j + hi], T.sem["ra%d%s" % (j, tail)]
+    return T.B_all[:, BW * i + lo:BW * i + hi], T.sem["rb" + tail]
 
 
 def rank_program(g, core, T, topo):
@@ -66,69 +77,85 @@ def rank_program(g, core, T, topo):
             if relay != core:
                 continue
             dst = cores[d]
-            out, arrived = _landing(T, kind, s)
             rid, pid, _ = topo.addr(dst)
-            g.wait_ge(sem.rx, NE_ON)
-            g.remote_dma(out_ap=out, in_ap=(T.a_d if kind == "a" else T.b_d)[:, :], remote_sem=arrived,
-                         local_sem=sem.sent, pid=pid, routing_id=rid,
-                         dma_engine_mask=_engines(topo.mask(core, dst), NE_OFF))
-            g.wait_ge(sem.sent, NE_OFF)
+            for piece in (0, 1):
+                out, arrived = _landing(T, kind, s, piece)
+                g.wait_ge(sem["rx%d" % piece], NE_IN[piece])
+                g.remote_dma(out_ap=out, in_ap=T["%s%d_d" % (kind, piece)][:, :], remote_sem=arrived,
+                             local_sem=sem.sent, pid=pid, routing_id=rid,
+                             dma_engine_mask=_pick(topo.mask(core, dst), NE_OFF))
+            g.wait_ge(sem.sent, 2 * NE_OFF)
         return
 
     i, j = divmod(rank, GC)
     mine = [f for f in flows if f[1] == rank]
+    relayed = [f for f in mine if f[3] is not None]
 
-    g.sync.dma_start(T.a_d[:, :], T.a[:, :]).then_inc(sem.la, 16)
-    g.scalar.dma_start(T.b_d[:, :], T.b[:, :]).then_inc(sem.lb, 16)
+    g.sync.dma_start(T.a0_d[:, :], T.a[:, CUT["a"][0]:CUT["a"][1]]).then_inc(sem.la0, 16)
+    g.scalar.dma_start(T.b0_d[:, :], T.b[:, CUT["b"][0]:CUT["b"][1]]).then_inc(sem.lb0, 16)
+    g.sync.dma_start(T.a1_d[:, :], T.a[:, CUT["a"][1]:CUT["a"][2]]).then_inc(sem.la1, 16)
+    g.scalar.dma_start(T.b1_d[:, :], T.b[:, CUT["b"][1]:CUT["b"][2]]).then_inc(sem.lb1, 16)
     g.sync.dma_start(T.A_all[:, AW * j:AW * (j + 1)], T.a[:, :]).then_inc(sem.las, 16)
     g.scalar.dma_start(T.B_all[:, BW * i:BW * (i + 1)], T.b[:, :]).then_inc(sem.lbs, 16)
 
+    def handing(group, piece):
+        used, hand = 0, []
+        for kind, s, d, relay in group:
+            rid, pid, _ = topo.addr(relay)
+            m = _pick(topo.mask(core, relay), NE_IN[piece], used)
+            used |= m
+            buf = T["%s%d_d" % (kind, piece)]
+            hand.append(RemoteDMATransfer(dst_ids=[DstId(rid=rid, pnc=pid)], dma_engine_mask=m,
+                                          remote_sem=sem["rx%d" % piece], src=buf[:, :], dst=buf[:, :]))
+        g.remote_dma_fused(hand, local_sem=sem.sent)
+        return NE_IN[piece] * len(group)
+
     sent = 0
-    g.wait_ge(sem.la, 16)
-    hand = []
-    for n, (kind, s, d, relay) in enumerate([f for f in mine if f[0] == "a" and f[3] is not None]):
-        rid, pid, _ = topo.addr(relay)
-        hand.append(RemoteDMATransfer(dst_ids=[DstId(rid=rid, pnc=pid)],
-                                      dma_engine_mask=_engines(topo.mask(core, relay), NE_ON, skip=n * NE_ON),
-                                      remote_sem=sem.rx, src=T.a_d[:, :], dst=T.a_d[:, :]))
-        sent += NE_ON
-    g.remote_dma_fused(hand, local_sem=sem.sent)
-    g.wait_ge(sem.lb, 16)
-    for kind, s, d, relay in [f for f in mine if f[0] == "b"]:
-        rid, pid, _ = topo.addr(relay)
-        g.remote_dma(out_ap=T.b_d[:, :], in_ap=T.b_d[:, :], remote_sem=sem.rx, local_sem=sem.sent, pid=pid,
-                     routing_id=rid, dma_engine_mask=_engines(topo.mask(core, relay), NE_ON))
-        sent += NE_ON
+    g.wait_ge(sem.la0, 16)
+    g.wait_ge(sem.lb0, 16)
+    sent += handing(relayed, 0)
+    g.wait_ge(sem.la1, 16)
+    sent += handing([f for f in relayed if f[0] == "a"], 1)
+    g.wait_ge(sem.lb1, 16)
+    sent += handing([f for f in relayed if f[0] == "b"], 1)
     for kind, s, d, relay in [f for f in mine if f[3] is None]:
         dst = cores[d]
-        out, arrived = _landing(T, kind, s)
+        out, arrived = _landing(T, kind, s, None)
         rid, pid, _ = topo.addr(dst)
-        g.remote_dma(out_ap=out, in_ap=T.a_d[:, :], remote_sem=arrived, local_sem=sem.sent, pid=pid,
-                     routing_id=rid, dma_engine_mask=_engines(topo.mask(core, dst), NE_OFF))
+        g.wait_ge(sem.las, 16)
+        g.remote_dma(out_ap=out, in_ap=T.A_all[:, AW * j:AW * (j + 1)], remote_sem=arrived, local_sem=sem.sent,
+                     pid=pid, routing_id=rid, dma_engine_mask=_pick(topo.mask(core, dst), NE_OFF))
         sent += NE_OFF
 
     how = {}
     for kind, s, d, relay in flows:
         if d == rank:
             how[(kind, s)] = relay
+
+    def sources(kind, s, t):
+        if s == rank:
+            return [(0, (kind, s, None), (sem.las if kind == "a" else sem.lbs), 16)]
+        if how[(kind, s)] is None:
+            return [(1, (kind, s, None), _landing(T, kind, s, None)[1], NE_OFF)]
+        width = P if kind == "a" else F
+        found = []
+        for piece in (0, 1):
+            if t * width < CUT[kind][piece + 1] and (t + 1) * width > CUT[kind][piece]:
+                stage = 2 if piece == 0 else (3 if kind == "b" else 4)
+                found.append((stage, (kind, s, piece), _landing(T, kind, s, piece)[1], NE_OFF))
+        return found
+
     need = {}
     for k in range(L):
-        sa, sb = i * GC + k // KA, (k // KB) * GC + j
-        stage_a = 0 if sa == rank else (1 if how[("a", sa)] is None else 2)
-        stage_b = 0 if sb == rank else 3
-        need[k] = (max(stage_a, stage_b), k, sa, sb)
-    order = sorted(range(L), key=lambda k: need[k][:2])
+        need[k] = sources("a", i * GC + k // KA, k % KA) + sources("b", (k // KB) * GC + j, k % KB)
+    order = sorted(range(L), key=lambda k: (max(w[0] for w in need[k]), k))
     waited = []
     for n, k in enumerate(order):
-        _, _, sa, sb = need[k]
-        for kind, s in (("a", sa), ("b", sb)):
-            if (kind, s) in waited:
+        for _, key, s_, count in need[k]:
+            if key in waited:
                 continue
-            waited.append((kind, s))
-            if s == rank:
-                g.tensor.wait_ge(sem.las if kind == "a" else sem.lbs, 16)
-            else:
-                g.tensor.wait_ge(_landing(T, kind, s)[1], NE_OFF)
+            waited.append(key)
+            g.tensor.wait_ge(s_, count)
         mm = g.tensor.matmul(T.acc[:, :], T.A_all[:, P * k:P * (k + 1)], T.B_all[:, F * k:F * (k + 1)],
                              n == 0, n == L - 1)
     mm.then_inc(sem.mm, 1)

from concourse.bass import DstId, RemoteDMATransfer

GR, GC = 2, 3
L, KA, KB, F = 12, 4, 6, 64
P = 128
AW, BW = KA * P, KB * F
HEAD = 64
CUT = {"a": (0, HEAD, AW), "b": (0, HEAD, BW)}

NE_IN = (4, 8)
NE_OFF = 8

SCRATCH = {
    "a0_d": ("dram", [P, HEAD], "bfloat16"),
    "a1_d": ("dram", [P, AW - HEAD], "bfloat16"),
    "b0_d": ("dram", [P, HEAD], "bfloat16"),
    "b1_d": ("dram", [P, BW - HEAD], "bfloat16"),
    "A_all": ("sbuf", [P, L * P], "bfloat16"),
    "B_all": ("sbuf", [P, L * F], "bfloat16"),
    "acc": ("psum", [P, F], "float32"),
    "y_s": ("sbuf", [P, F], "bfloat16"),
}
SEMAPHORES = ["la0", "la1", "lb0", "lb1", "las", "lbs", "rx0", "rx1",
              "ra0h", "ra1h", "ra2h", "ra0", "ra1", "ra2", "rbh", "rb", "sent", "mm", "cp", "st"]


def _pick(mask, n, used=0):
    bits = [e for e in range(mask.bit_length()) if (mask >> e) & 1 and not (used >> e) & 1]
    return sum(1 << e for e in bits[len(bits) - n:])


def _flows(cores, topo):
    everyone = range(topo.CHIPS * topo.CORES_PER_CHIP)
    flows = []
    for s, src in enumerate(cores):
        i, j = divmod(s, GC)
        wanted = [("a", i * GC + jj, min(j, jj) == 0) for jj in range(GC) if jj != j]
        wanted.append(("b", (1 - i) * GC + j, j == GC - 1))
        taken = []
        for kind, d, other_die in wanted:
            dst = cores[d]
            if topo.may_write(src, dst):
                flows.append((kind, s, d, None))
                continue
            if kind == "b" and 0 < j < GC - 1:
                able = [h for h in everyone
                        if topo.mates(topo.chip(h), topo.chip(dst)) and h not in cores
                        and topo.may_write(src, h) and topo.may_write(h, dst)]
            else:
                able = [h for h in everyone
                        if topo.chip(h) == topo.chip(src) and h not in cores and h not in taken
                        and topo.may_write(h, dst)]
            liked = [h for h in able if (topo.die(h) != topo.die(src)) == other_die]
            relay = (liked or able)[0]
            taken.append(relay)
            flows.append((kind, s, d, relay))
    return flows


def _landing(T, kind, s, piece):
    i, j = divmod(s, GC)
    lo, hi = (CUT[kind][0], CUT[kind][2]) if piece is None else (CUT[kind][piece], CUT[kind][piece + 1])
    tail = "h" if piece == 0 else ""
    if kind == "a":
        return T.A_all[:, AW * j + lo:AW * j + hi], T.sem["ra%d%s" % (j, tail)]
    return T.B_all[:, BW * i + lo:BW * i + hi], T.sem["rb" + tail]


def rank_program(g, core, T, topo):
    cores = list(T.cores)
    flows = _flows(cores, topo)
    sem = T.sem
    rank = T.rank_of(core)

    if rank is None:
        for kind, s, d, relay in flows:
            if relay != core:
                continue
            dst = cores[d]
            rid, pid, _ = topo.addr(dst)
            for piece in (0, 1):
                out, arrived = _landing(T, kind, s, piece)
                g.wait_ge(sem["rx%d" % piece], NE_IN[piece])
                g.remote_dma(out_ap=out, in_ap=T["%s%d_d" % (kind, piece)][:, :], remote_sem=arrived,
                             local_sem=sem.sent, pid=pid, routing_id=rid,
                             dma_engine_mask=_pick(topo.mask(core, dst), NE_OFF))
            g.wait_ge(sem.sent, 2 * NE_OFF)
        return

    i, j = divmod(rank, GC)
    mine = [f for f in flows if f[1] == rank]
    relayed = [f for f in mine if f[3] is not None]

    g.sync.dma_start(T.a0_d[:, :], T.a[:, CUT["a"][0]:CUT["a"][1]]).then_inc(sem.la0, 16)
    g.scalar.dma_start(T.b0_d[:, :], T.b[:, CUT["b"][0]:CUT["b"][1]]).then_inc(sem.lb0, 16)
    g.sync.dma_start(T.a1_d[:, :], T.a[:, CUT["a"][1]:CUT["a"][2]]).then_inc(sem.la1, 16)
    g.scalar.dma_start(T.b1_d[:, :], T.b[:, CUT["b"][1]:CUT["b"][2]]).then_inc(sem.lb1, 16)
    g.sync.dma_start(T.A_all[:, AW * j:AW * (j + 1)], T.a[:, :]).then_inc(sem.las, 16)
    g.scalar.dma_start(T.B_all[:, BW * i:BW * (i + 1)], T.b[:, :]).then_inc(sem.lbs, 16)

    def handing(group, piece):
        used, hand = 0, []
        for kind, s, d, relay in group:
            rid, pid, _ = topo.addr(relay)
            m = _pick(topo.mask(core, relay), NE_IN[piece], used)
            used |= m
            buf = T["%s%d_d" % (kind, piece)]
            hand.append(RemoteDMATransfer(dst_ids=[DstId(rid=rid, pnc=pid)], dma_engine_mask=m,
                                          remote_sem=sem["rx%d" % piece], src=buf[:, :], dst=buf[:, :]))
        g.remote_dma_fused(hand, local_sem=sem.sent)
        return NE_IN[piece] * len(group)

    sent = 0
    g.wait_ge(sem.la0, 16)
    g.wait_ge(sem.lb0, 16)
    sent += handing(relayed, 0)
    g.wait_ge(sem.la1, 16)
    sent += handing([f for f in relayed if f[0] == "a"], 1)
    g.wait_ge(sem.lb1, 16)
    sent += handing([f for f in relayed if f[0] == "b"], 1)
    for kind, s, d, relay in [f for f in mine if f[3] is None]:
        dst = cores[d]
        out, arrived = _landing(T, kind, s, None)
        rid, pid, _ = topo.addr(dst)
        g.wait_ge(sem.las, 16)
        g.remote_dma(out_ap=out, in_ap=T.A_all[:, AW * j:AW * (j + 1)], remote_sem=arrived, local_sem=sem.sent,
                     pid=pid, routing_id=rid, dma_engine_mask=_pick(topo.mask(core, dst), NE_OFF))
        sent += NE_OFF

    how = {}
    for kind, s, d, relay in flows:
        if d == rank:
            how[(kind, s)] = relay

    def sources(kind, s, t):
        if s == rank:
            return [(0, (kind, s, None), (sem.las if kind == "a" else sem.lbs), 16)]
        if how[(kind, s)] is None:
            return [(1, (kind, s, None), _landing(T, kind, s, None)[1], NE_OFF)]
        width = P if kind == "a" else F
        found = []
        for piece in (0, 1):
            if t * width < CUT[kind][piece + 1] and (t + 1) * width > CUT[kind][piece]:
                stage = 2 if piece == 0 else (3 if kind == "b" else 4)
                found.append((stage, (kind, s, piece), _landing(T, kind, s, piece)[1], NE_OFF))
        return found

    need = {}
    for k in range(L):
        need[k] = sources("a", i * GC + k // KA, k % KA) + sources("b", (k // KB) * GC + j, k % KB)
    order = sorted(range(L), key=lambda k: (max(w[0] for w in need[k]), k))
    waited = []
    for n, k in enumerate(order):
        for _, key, s_, count in need[k]:
            if key in waited:
                continue
            waited.append(key)
            g.tensor.wait_ge(s_, count)
        mm = g.tensor.matmul(T.acc[:, :], T.A_all[:, P * k:P * (k + 1)], T.B_all[:, F * k:F * (k + 1)],
                             n == 0, n == L - 1)
    mm.then_inc(sem.mm, 1)

    g.vector.wait_ge(sem.mm, 1)
    g.vector.tensor_copy(T.y_s[:, :], T.acc[:, :]).then_inc(sem.cp, 1)
    g.sync.wait_ge(sem.cp, 1)
    g.sync.dma_start(T.y[:, :], T.y_s[:, :]).then_inc(sem.st, 16)
    g.sync.wait_ge(sem.st, 16)
    g.wait_ge(sem.sent, sent)
